import numpy as np, ml_dtypes
CORES = [129,145,193,257,273,321,385,401,449]
N = 9
TK = 64
def setup_inputs(rng):
    return {"x": rng.standard_normal((N, 128, N * TK), dtype=np.float32).astype(ml_dtypes.bfloat16), "t": rng.standard_normal((N, 128, N * TK), dtype=np.float32).astype(ml_dtypes.bfloat16), "f1": (rng.standard_normal((N, 128, 128), dtype=np.float32) / 11).astype(ml_dtypes.bfloat16), "f2": (rng.standard_normal((N, 128, 128), dtype=np.float32) / 11).astype(ml_dtypes.bfloat16)}
def setup_inputs_big(rng):
    d = setup_inputs(rng)
    for k in ("x", "t", "f1", "f2"): d[k] = (d[k].astype(np.float32) * 1024.0).astype(d[k].dtype)
    return d
def setup_inputs_small(rng):
    d = setup_inputs(rng)
    for k in ("x", "t", "f1", "f2"): d[k] = (d[k].astype(np.float32) * (1 / 1024.0)).astype(d[k].dtype)
    return d
def reference(x, t, f1, f2):
    X, T, F1, F2 = x.astype(np.float64), t.astype(np.float64), f1.astype(np.float64), f2.astype(np.float64)
    y = np.zeros((N, 128, N * TK))
    for j in range(N):
        u = (F1[j].T @ X[j]) * T[j]
        for r in range(N):
            y[r][:, TK * j:TK * j + TK] = F2[r].T @ u[:, TK * r:TK * r + TK]
    return {"y": y.astype(ml_dtypes.bfloat16)}

@@ -1,0 +1,171 @@
+from concourse.bass import DstId, RemoteDMATransfer
+from concourse.mybir import AluOpType
+
+N = 9
+TK = 64
+WORLD = 512
+NG = 3
+GW = 3 * TK
+
+SCRATCH = {
+    "xs": ("sbuf", [128, N * TK], "bfloat16"),
+    "ts": ("sbuf", [128, N * TK], "bfloat16"),
+    "f1s": ("sbuf", [128, 128], "bfloat16"),
+    "f2s": ("sbuf", [128, 128], "bfloat16"),
+    "u": ("sbuf", [128, N * TK], "bfloat16"),
+    "rx": ("sbuf", [128, N * TK], "bfloat16"),
+    "ys": ("sbuf", [128, N * TK], "bfloat16"),
+    "pv0": ("psum", [128, 512], "float32"), "pv1": ("psum", [128, 512], "float32"), "pv2": ("psum", [128, 512], "float32"),
+    "py0": ("psum", [128, 512], "float32"), "py1": ("psum", [128, 512], "float32"), "py2": ("psum", [128, 512], "float32"),
+}
+SEMAPHORES = (["ldx", "ldf1", "ldt", "ldf2", "rl", "sent"]
+              + ["%s%d" % (n, k) for n in ("mm", "u", "arr", "ym", "yc", "st") for k in range(NG)])
+
+
+def _bits(mask):
+    return [b for b in range(16) if (mask >> b) & 1]
+
+
+def _pack(n, engines):
+    out = []
+    while n:
+        k = 1
+        while k * 2 <= n and k * 2 <= engines:
+            k *= 2
+        out.append([engines // k] * k)
+        n -= k
+    return out
+
+
+def _pick_helper(topo, src, dsts, taken):
+    for k in range(WORLD):
+        if k in taken or not topo.may_write(src, k):
+            continue
+        if topo.chip(k) != topo.chip(src) or topo.rack(topo.host(k)) == topo.rack(topo.host(src)):
+            continue
+        if not all(topo.same_plane(k, d) and topo.may_write(k, d) for d in dsts):
+            continue
+        if topo.die(k) == topo.die(dsts[0]):
+            continue
+        return k
+    raise ValueError("no helper")
+
+
+def _plan(T, topo):
+    cores = list(T.cores)
+    hosts = sorted({topo.host(c) for c in cores})
+    groups = [[j for j in range(N) if topo.host(cores[j]) == h] for h in hosts]
+    calls, expect, send_order, recv_order = {}, {}, {}, {}
+    taken = set(cores)
+
+    def add_calls(core, singles):
+        eng = len(_bits(topo.mask(core, singles[0][1])))
+        at = 0
+        for shape in _pack(len(singles), eng):
+            part = singles[at:at + len(shape)]
+            at += len(shape)
+            waits = sorted({w for s in part for w in s[0]})
+            calls.setdefault(core, []).append((waits, [(s[1], s[2], s[2] + TK, s[3], e, s[4]) for s, e in zip(part, shape)]))
+
+    for j, c in enumerate(cores):
+        own = [g for g in range(NG) if j in groups[g]][0]
+        others = [g for g in range(NG) if g != own]
+        far = [g for g in others if not all(topo.may_write(c, cores[r]) for r in groups[g])]
+        near = [g for g in others if g not in far]
+        send_order[j] = far + near + [own]
+        recv_order[j] = ([own] + near + far) if far else (near + [own])
+        for g in far:
+            dsts = [cores[r] for r in groups[g]]
+            h = _pick_helper(topo, c, dsts, taken)
+            taken.add(h)
+            lo, hi = TK * groups[g][0], TK * (groups[g][-1] + 1)
+            eng = len(_bits(topo.mask(c, h)))
+            calls.setdefault(c, []).append(([("u%d" % g, 1)], [(h, lo, hi, lo, eng, "rl")]))
+            add_calls(h, [([("rl", eng)], cores[r], TK * r, TK * j, "arr%d" % own) for r in groups[g]])
+        add_calls(c, [([("u%d" % g, 1)], cores[r], TK * r, TK * j, "arr%d" % own)
+                      for g in near + [own] for r in groups[g] if r != j])
+    for c in calls:
+        for _, writes in calls[c]:
+            for d, _, _, _, e, s in writes:
+                expect.setdefault(d, {})
+                expect[d][s] = expect[d].get(s, 0) + e
+    return groups, calls, expect, send_order, recv_order
+
+
+def _issue(g, core, T, topo, calls, src):
+    sent = 0
+    used = {}
+    for waits, writes in calls:
+        for s, v in waits:
+            g.wait_ge(T.sem[s], v)
+        free = sorted(_bits(topo.mask(core, writes[0][0])), key=lambda b: (used.get(b, 0), b))
+        trs = []
+        for d, lo, hi, dlo, e, s in writes:
+            mine, free = free[:e], free[e:]
+            m = 0
+            for b in mine:
+                m |= 1 << b
+                used[b] = used.get(b, 0) + 128 // e
+            rid, pid = topo.addr(d, core)
+            trs.append((d, rid, pid, m, lo, hi, dlo, s))
+            sent += e
+        if len(trs) == 1:
+            d, rid, pid, m, lo, hi, dlo, s = trs[0]
+            g.remote_dma(out_ap=T.rx[:, dlo:dlo + hi - lo], in_ap=src[:, lo:hi], remote_sem=T.sem[s], local_sem=T.sem.sent,
+                         pid=pid, routing_id=rid, dma_engine_mask=m)
+        else:
+            g.remote_dma_fused([RemoteDMATransfer(dst_ids=[DstId(rid=rid, pnc=pid)], dma_engine_mask=m, remote_sem=T.sem[s],
+                                                  src=src[:, lo:hi], dst=T.rx[:, dlo:dlo + hi - lo])
+                                for d, rid, pid, m, lo, hi, dlo, s in trs], local_sem=T.sem.sent)
+    g.wait_ge(T.sem.sent, sent)
+
+
+def rank_program(g, core, T, topo):
+    groups, calls, expect, send_order, recv_order = _plan(T, topo)
+    j = T.rank_of(core)
+    if j is None:
+        if core in calls:
+            _issue(g, core, T, topo, calls[core], T.rx)
+        return
+    sem = T.sem
+    own = [k for k in range(NG) if j in groups[k]][0]
+
+    g.sync.dma_start(T.xs[:], T.x[:]).then_inc(sem.ldx, 16)
+    g.scalar.dma_start(T.f1s[:], T.f1[:]).then_inc(sem.ldf1, 16)
+    g.scalar.dma_start(T.ts[:], T.t[:]).then_inc(sem.ldt, 16)
+    g.sync.dma_start(T.f2s[:], T.f2[:]).then_inc(sem.ldf2, 16)
+
+    g.tensor.wait_ge(sem.ldx, 16)
+    g.tensor.wait_ge(sem.ldf1, 16)
+    g.vector.wait_ge(sem.ldt, 16)
+    for k in send_order[j]:
+        lo, hi = TK * groups[k][0], TK * (groups[k][-1] + 1)
+        pv = T["pv%d" % k]
+        g.tensor.matmul(pv[:, 0:hi - lo], T.f1s[:], T.xs[:, lo:hi], True, True).then_inc(sem["mm%d" % k], 1)
+        g.vector.wait_ge(sem["mm%d" % k], 1)
+        g.vector.tensor_tensor(T.u[:, lo:hi], pv[:, 0:hi - lo], T.ts[:, lo:hi], AluOpType.mult).then_inc(sem["u%d" % k], 1)
+
+    _issue(g, core, T, topo, calls[core], T.u)
+
+    g.tensor.wait_ge(sem.ldf2, 16)
+    queues = [g.sync, g.scalar]
+    for n, k in enumerate(recv_order[j]):
+        lo, hi = TK * groups[k][0], TK * (groups[k][-1] + 1)
+        py = T["py%d" % k]
+        g.tensor.wait_ge(sem["arr%d" % k], expect[core]["arr%d" % k])
+        if k == own:
+            g.tensor.wait_ge(sem["u%d" % k], 1)
+            for r in groups[k]:
+                rhs = T.u if r == j else T.rx
+                g.tensor.matmul(py[:, TK * r - lo:TK * r - lo + TK], T.f2s[:], rhs[:, TK * r:TK * r + TK], True, True).then_inc(sem["ym%d" % k], 1)
+            done = len(groups[k])
+        else:
+            g.tensor.matmul(py[:, 0:hi - lo], T.f2s[:], T.rx[:, lo:hi], True, True).then_inc(sem["ym%d" % k], 1)
+            done = 1
+        g.vector.wait_ge(sem["ym%d" % k], done)
+        g.vector.tensor_copy(T.ys[:, lo:hi], py[:, 0:hi - lo]).then_inc(sem["yc%d" % k], 1)
+        q = queues[n % 2]
+        q.wait_ge(sem["yc%d" % k], 1)
+        q.dma_start(T.y[:, lo:hi], T.ys[:, lo:hi]).then_inc(sem["st%d" % k], 16)
+    for n, k in enumerate(recv_order[j]):
+        queues[n % 2].wait_ge(sem["st%d" % k], 16)

@@ -4,8 +4,7 @@ from concourse.mybir import AluOpType
 N = 9
 TK = 64
 WORLD = 512
-NG = 3
-GW = 3 * TK
+NB = 8
 
 SCRATCH = {
     "xs": ("sbuf", [128, N * TK], "bfloat16"),
@@ -15,11 +14,16 @@ SCRATCH = {
     "u": ("sbuf", [128, N * TK], "bfloat16"),
     "rx": ("sbuf", [128, N * TK], "bfloat16"),
     "ys": ("sbuf", [128, N * TK], "bfloat16"),
-    "pv0": ("psum", [128, 512], "float32"), "pv1": ("psum", [128, 512], "float32"), "pv2": ("psum", [128, 512], "float32"),
-    "py0": ("psum", [128, 512], "float32"), "py1": ("psum", [128, 512], "float32"), "py2": ("psum", [128, 512], "float32"),
 }
-SEMAPHORES = (["ldx", "ldf1", "ldt", "ldf2", "rl", "sent"]
-              + ["%s%d" % (n, k) for n in ("mm", "u", "arr", "ym", "yc", "st") for k in range(NG)])
+for _b in range(NB):
+    SCRATCH["ps%d" % _b] = ("psum", [128, 512], "float32")
+SEMAPHORES = (["lf1", "lf2", "rl", "sent"]
+              + ["%s%d" % (n, k) for n in ("lx", "lt", "mm", "u") for k in range(4)]
+              + ["arr%d" % k for k in range(N)]
+              + ["ym%d" % k for k in range(6)]
+              + ["%s%d" % (n, k) for n in ("yc", "st") for k in range(4)])
+
+_CACHE = {}
 
 
 def _bits(mask):
@@ -29,6 +33,9 @@ def _bits(mask):
 def _pack(n, engines):
     out = []
     while n:
+        if n == 3 and engines >= 4:
+            out.append([engines // 4, engines // 4, engines // 2])
+            break
         k = 1
         while k * 2 <= n and k * 2 <= engines:
             k *= 2
@@ -55,7 +62,8 @@ def _plan(T, topo):
     cores = list(T.cores)
     hosts = sorted({topo.host(c) for c in cores})
     groups = [[j for j in range(N) if topo.host(cores[j]) == h] for h in hosts]
-    calls, expect, send_order, recv_order = {}, {}, {}, {}
+    calls, expect = {}, {}
+    pieces, loads, pload, units, ownp = {}, {}, {}, {}, {}
     taken = set(cores)
 
     def add_calls(core, singles):
@@ -68,28 +76,53 @@ def _plan(T, topo):
             calls.setdefault(core, []).append((waits, [(s[1], s[2], s[2] + TK, s[3], e, s[4]) for s, e in zip(part, shape)]))
 
     for j, c in enumerate(cores):
-        own = [g for g in range(NG) if j in groups[g]][0]
-        others = [g for g in range(NG) if g != own]
+        own = [g for g in range(len(groups)) if j in groups[g]][0]
+        others = [g for g in range(len(groups)) if g != own]
         far = [g for g in others if not all(topo.may_write(c, cores[r]) for r in groups[g])]
         near = [g for g in others if g not in far]
-        send_order[j] = far + near + [own]
-        recv_order[j] = ([own] + near + far) if far else (near + [own])
+        pc, ld, pl = [], [], []
         for g in far:
-            dsts = [cores[r] for r in groups[g]]
-            h = _pick_helper(topo, c, dsts, taken)
-            taken.add(h)
-            lo, hi = TK * groups[g][0], TK * (groups[g][-1] + 1)
-            eng = len(_bits(topo.mask(c, h)))
-            calls.setdefault(c, []).append(([("u%d" % g, 1)], [(h, lo, hi, lo, eng, "rl")]))
-            add_calls(h, [([("rl", eng)], cores[r], TK * r, TK * j, "arr%d" % own) for r in groups[g]])
-        add_calls(c, [([("u%d" % g, 1)], cores[r], TK * r, TK * j, "arr%d" % own)
-                      for g in near + [own] for r in groups[g] if r != j])
+            b = groups[g]
+            for lo, hi in ((b[0], b[0] + 2), (b[0] + 2, b[-1] + 1)):
+                p = len(pc)
+                pc.append((lo, hi))
+                pl.append(len(ld))
+                ld.append((lo, hi))
+                h = _pick_helper(topo, c, [cores[r] for r in range(lo, hi)], taken)
+                taken.add(h)
+                eng = len(_bits(topo.mask(c, h)))
+                calls.setdefault(c, []).append(([("u%d" % p, 1)], [(h, TK * lo, TK * hi, TK * lo, eng, "rl")]))
+                add_calls(h, [([("rl", eng)], cores[r], TK * r, TK * j, "arr%d" % j) for r in range(lo, hi)])
+        rest = near + [own]
+        blocks = sorted(r for g in rest for r in groups[g])
+        merged = bool(far) and blocks == list(range(blocks[0], blocks[-1] + 1))
+        if merged:
+            ld.append((blocks[0], blocks[-1] + 1))
+        gp = {}
+        for g in rest:
+            b = groups[g]
+            gp[g] = len(pc)
+            pc.append((b[0], b[-1] + 1))
+            if merged:
+                pl.append(len(ld) - 1)
+            else:
+                pl.append(len(ld))
+                ld.append((b[0], b[-1] + 1))
+        singles = {g: [([("u%d" % gp[g], 1)], cores[r], TK * r, TK * j, "arr%d" % j) for r in groups[g] if r != j]
+                   for g in rest}
+        if far:
+            add_calls(c, [s for g in rest for s in singles[g]])
+        else:
+            for g in rest:
+                add_calls(c, singles[g])
+        pieces[j], loads[j], pload[j], ownp[j] = pc, ld, pl, gp[own]
+        units[j] = [(groups[g], False) for g in near] + [(groups[own], False)] + [(groups[g], True) for g in far]
     for c in calls:
         for _, writes in calls[c]:
             for d, _, _, _, e, s in writes:
                 expect.setdefault(d, {})
                 expect[d][s] = expect[d].get(s, 0) + e
-    return groups, calls, expect, send_order, recv_order
+    return {"calls": calls, "expect": expect, "pieces": pieces, "loads": loads, "pload": pload, "units": units, "ownp": ownp}
 
 
 def _issue(g, core, T, topo, calls, src):
@@ -121,51 +154,85 @@ def _issue(g, core, T, topo, calls, src):
 
 
 def rank_program(g, core, T, topo):
-    groups, calls, expect, send_order, recv_order = _plan(T, topo)
+    if "p" not in _CACHE:
+        _CACHE["p"] = _plan(T, topo)
+    P = _CACHE["p"]
+    calls, expect = P["calls"], P["expect"]
     j = T.rank_of(core)
     if j is None:
         if core in calls:
             _issue(g, core, T, topo, calls[core], T.rx)
         return
     sem = T.sem
-    own = [k for k in range(NG) if j in groups[k]][0]
+    pieces, loads, pload, units, ownp = P["pieces"][j], P["loads"][j], P["pload"][j], P["units"][j], P["ownp"][j]
 
-    g.sync.dma_start(T.xs[:], T.x[:]).then_inc(sem.ldx, 16)
-    g.scalar.dma_start(T.f1s[:], T.f1[:]).then_inc(sem.ldf1, 16)
-    g.scalar.dma_start(T.ts[:], T.t[:]).then_inc(sem.ldt, 16)
-    g.sync.dma_start(T.f2s[:], T.f2[:]).then_inc(sem.ldf2, 16)
+    g.scalar.dma_start(T.f1s[:], T.f1[:]).then_inc(sem.lf1, 16)
+    for n, (lo, hi) in enumerate(loads):
+        g.sync.dma_start(T.xs[:, TK * lo:TK * hi], T.x[:, TK * lo:TK * hi]).then_inc(sem["lx%d" % n], 16)
+        g.scalar.dma_start(T.ts[:, TK * lo:TK * hi], T.t[:, TK * lo:TK * hi]).then_inc(sem["lt%d" % n], 16)
+    g.sync.dma_start(T.f2s[:], T.f2[:]).then_inc(sem.lf2, 16)
 
-    g.tensor.wait_ge(sem.ldx, 16)
-    g.tensor.wait_ge(sem.ldf1, 16)
-    g.vector.wait_ge(sem.ldt, 16)
-    for k in send_order[j]:
-        lo, hi = TK * groups[k][0], TK * (groups[k][-1] + 1)
-        pv = T["pv%d" % k]
-        g.tensor.matmul(pv[:, 0:hi - lo], T.f1s[:], T.xs[:, lo:hi], True, True).then_inc(sem["mm%d" % k], 1)
-        g.vector.wait_ge(sem["mm%d" % k], 1)
-        g.vector.tensor_tensor(T.u[:, lo:hi], pv[:, 0:hi - lo], T.ts[:, lo:hi], AluOpType.mult).then_inc(sem["u%d" % k], 1)
+    g.tensor.wait_ge(sem.lf1, 16)
+    seen = set()
+    for p, (lo, hi) in enumerate(pieces):
+        n = pload[p]
+        if n not in seen:
+            seen.add(n)
+            g.tensor.wait_ge(sem["lx%d" % n], 16)
+            g.vector.wait_ge(sem["lt%d" % n], 16)
+        ps, w = T["ps%d" % p], TK * (hi - lo)
+        g.tensor.matmul(ps[:, 0:w], T.f1s[:], T.xs[:, TK * lo:TK * hi], True, True).then_inc(sem["mm%d" % p], 1)
+        g.vector.wait_ge(sem["mm%d" % p], 1)
+        g.vector.tensor_tensor(T.u[:, TK * lo:TK * hi], ps[:, 0:w], T.ts[:, TK * lo:TK * hi], AluOpType.mult).then_inc(sem["u%d" % p], 1)
 
     _issue(g, core, T, topo, calls[core], T.u)
 
-    g.tensor.wait_ge(sem.ldf2, 16)
+    g.tensor.wait_ge(sem.lf2, 16)
     queues = [g.sync, g.scalar]
-    for n, k in enumerate(recv_order[j]):
-        lo, hi = TK * groups[k][0], TK * (groups[k][-1] + 1)
-        py = T["py%d" % k]
-        g.tensor.wait_ge(sem["arr%d" % k], expect[core]["arr%d" % k])
-        if k == own:
-            g.tensor.wait_ge(sem["u%d" % k], 1)
-            for r in groups[k]:
-                rhs = T.u if r == j else T.rx
-                g.tensor.matmul(py[:, TK * r - lo:TK * r - lo + TK], T.f2s[:], rhs[:, TK * r:TK * r + TK], True, True).then_inc(sem["ym%d" % k], 1)
-            done = len(groups[k])
+    bank, ym = [len(pieces)], [0]
+
+    def next_bank():
+        b = bank[0]
+        bank[0] += 1
+        if b >= NB:
+            b -= NB
+            g.tensor.wait_ge(sem["u%d" % b], 1)
+        return T["ps%d" % b]
+
+    for n, (blocks, blockwise) in enumerate(units):
+        lo, hi = TK * blocks[0], TK * (blocks[-1] + 1)
+        copies = 0
+        if blockwise:
+            for r in blocks:
+                py = next_bank()
+                k = ym[0]
+                ym[0] += 1
+                g.tensor.wait_ge(sem["arr%d" % r], expect[core]["arr%d" % r])
+                g.tensor.matmul(py[:, 0:TK], T.f2s[:], T.rx[:, TK * r:TK * r + TK], True, True).then_inc(sem["ym%d" % k], 1)
+                g.vector.wait_ge(sem["ym%d" % k], 1)
+                g.vector.tensor_copy(T.ys[:, TK * r:TK * r + TK], py[:, 0:TK]).then_inc(sem["yc%d" % n], 1)
+                copies += 1
         else:
-            g.tensor.matmul(py[:, 0:hi - lo], T.f2s[:], T.rx[:, lo:hi], True, True).then_inc(sem["ym%d" % k], 1)
-            done = 1
-        g.vector.wait_ge(sem["ym%d" % k], done)
-        g.vector.tensor_copy(T.ys[:, lo:hi], py[:, 0:hi - lo]).then_inc(sem["yc%d" % k], 1)
+            py = next_bank()
+            k = ym[0]
+            ym[0] += 1
+            for r in blocks:
+                if r != j:
+                    g.tensor.wait_ge(sem["arr%d" % r], expect[core]["arr%d" % r])
+            if j in blocks:
+                g.tensor.wait_ge(sem["u%d" % ownp], 1)
+                for r in blocks:
+                    rhs = T.u if r == j else T.rx
+                    g.tensor.matmul(py[:, TK * r - lo:TK * r - lo + TK], T.f2s[:], rhs[:, TK * r:TK * r + TK], True, True).then_inc(sem["ym%d" % k], 1)
+                done = len(blocks)
+            else:
+                g.tensor.matmul(py[:, 0:hi - lo], T.f2s[:], T.rx[:, lo:hi], True, True).then_inc(sem["ym%d" % k], 1)
+                done = 1
+            g.vector.wait_ge(sem["ym%d" % k], done)
+            g.vector.tensor_copy(T.ys[:, lo:hi], py[:, 0:hi - lo]).then_inc(sem["yc%d" % n], 1)
+            copies = 1
         q = queues[n % 2]
-        q.wait_ge(sem["yc%d" % k], 1)
-        q.dma_start(T.y[:, lo:hi], T.ys[:, lo:hi]).then_inc(sem["st%d" % k], 16)
-    for n, k in enumerate(recv_order[j]):
-        queues[n % 2].wait_ge(sem["st%d" % k], 16)
+        q.wait_ge(sem["yc%d" % n], copies)
+        q.dma_start(T.y[:, lo:hi], T.ys[:, lo:hi]).then_inc(sem["st%d" % n], 16)
+    for n in range(len(units)):
+        queues[n % 2].wait_ge(sem["st%d" % n], 16)

from concourse.bass import DstId, RemoteDMATransfer
from concourse.mybir import AluOpType

N = 9
TK = 64
WORLD = 512
NB = 8

SCRATCH = {
    "xs": ("sbuf", [128, N * TK], "bfloat16"),
    "ts": ("sbuf", [128, N * TK], "bfloat16"),
    "f1s": ("sbuf", [128, 128], "bfloat16"),
    "f2s": ("sbuf", [128, 128], "bfloat16"),
    "u": ("sbuf", [128, N * TK], "bfloat16"),
    "rx": ("sbuf", [128, N * TK], "bfloat16"),
    "ys": ("sbuf", [128, N * TK], "bfloat16"),
}
for _b in range(NB):
    SCRATCH["ps%d" % _b] = ("psum", [128, 512], "float32")
SEMAPHORES = (["lf1", "lf2", "rl", "sent"]
              + ["%s%d" % (n, k) for n in ("lx", "lt", "mm", "u") for k in range(4)]
              + ["arr%d" % k for k in range(N)]
              + ["ym%d" % k for k in range(6)]
              + ["%s%d" % (n, k) for n in ("yc", "st") for k in range(4)])

_CACHE = {}


def _bits(mask):
    return [b for b in range(16) if (mask >> b) & 1]


def _pack(n, engines):
    out = []
    while n:
        if n == 3 and engines >= 4:
            out.append([engines // 4, engines // 4, engines // 2])
            break
        k = 1
        while k * 2 <= n and k * 2 <= engines:
            k *= 2
        out.append([engines // k] * k)
        n -= k
    return out


def _pick_helper(topo, src, dsts, taken):
    for k in range(WORLD):
        if k in taken or not topo.may_write(src, k):
            continue
        if topo.chip(k) != topo.chip(src) or topo.rack(topo.host(k)) == topo.rack(topo.host(src)):
            continue
        if not all(topo.same_plane(k, d) and topo.may_write(k, d) for d in dsts):
            continue
        if topo.die(k) == topo.die(dsts[0]):
            continue
        return k
    raise ValueError("no helper")


def _plan(T, topo):
    cores = list(T.cores)
    hosts = sorted({topo.host(c) for c in cores})
    groups = [[j for j in range(N) if topo.host(cores[j]) == h] for h in hosts]
    calls, expect = {}, {}
    pieces, loads, pload, units, ownp = {}, {}, {}, {}, {}
    taken = set(cores)

    def add_calls(core, singles):
        eng = len(_bits(topo.mask(core, singles[0][1])))
        at = 0
        for shape in _pack(len(singles), eng):
            part = singles[at:at + len(shape)]
            at += len(shape)
            waits = sorted({w for s in part for w in s[0]})
            calls.setdefault(core, []).append((waits, [(s[1], s[2], s[2] + TK, s[3], e, s[4]) for s, e in zip(part, shape)]))

    for j, c in enumerate(cores):
        own = [g for g in range(len(groups)) if j in groups[g]][0]
        others = [g for g in range(len(groups)) if g != own]
        far = [g for g in others if not all(topo.may_write(c, cores[r]) for r in groups[g])]
        near = [g for g in others if g not in far]
        pc, ld, pl = [], [], []
        for g in far:
            b = groups[g]
            for lo, hi in ((b[0], b[0] + 2), (b[0] + 2, b[-1] + 1)):
                p = len(pc)
                pc.append((lo, hi))
                pl.append(len(ld))
                ld.append((lo, hi))
                h = _pick_helper(topo, c, [cores[r] for r in range(lo, hi)], taken)
                taken.add(h)
                eng = len(_bits(topo.mask(c, h)))
                calls.setdefault(c, []).append(([("u%d" % p, 1)], [(h, TK * lo, TK * hi, TK * lo, eng, "rl")]))
                add_calls(h, [([("rl", eng)], cores[r], TK * r, TK * j, "arr%d" % j) for r in range(lo, hi)])
        rest = near + [own]
        blocks = sorted(r for g in rest for r in groups[g])
        merged = bool(far) and blocks == list(range(blocks[0], blocks[-1] + 1))
        if merged:
            ld.append((blocks[0], blocks[-1] + 1))
        gp = {}
        for g in rest:
            b = groups[g]
            gp[g] = len(pc)
            pc.append((b[0], b[-1] + 1))
            if merged:
                pl.append(len(ld) - 1)
            else:
                pl.append(len(ld))
                ld.append((b[0], b[-1] + 1))
        singles = {g: [([("u%d" % gp[g], 1)], cores[r], TK * r, TK * j, "arr%d" % j) for r in groups[g] if r != j]
                   for g in rest}
        if far:
            add_calls(c, [s for g in rest for s in singles[g]])
        else:
            for g in rest:
                add_calls(c, singles[g])
        pieces[j], loads[j], pload[j], ownp[j] = pc, ld, pl, gp[own]
        units[j] = [(groups[g], False) for g in near] + [(groups[own], False)] + [(groups[g], True) for g in far]
    for c in calls:
        for _, writes in calls[c]:
            for d, _, _, _, e, s in writes:
                expect.setdefault(d, {})
                expect[d][s] = expect[d].get(s, 0) + e
    return {"calls": calls, "expect": expect, "pieces": pieces, "loads": loads, "pload": pload, "units": units, "ownp": ownp}


def _issue(g, core, T, topo, calls, src):
    sent = 0
    used = {}
    for waits, writes in calls:
        for s, v in waits:
            g.wait_ge(T.sem[s], v)
        free = sorted(_bits(topo.mask(core, writes[0][0])), key=lambda b: (used.get(b, 0), b))
        trs = []
        for d, lo, hi, dlo, e, s in writes:
            mine, free = free[:e], free[e:]
            m = 0
            for b in mine:
                m |= 1 << b
                used[b] = used.get(b, 0) + 128 // e
            rid, pid = topo.addr(d, core)
            trs.append((d, rid, pid, m, lo, hi, dlo, s))
            sent += e
        if len(trs) == 1:
            d, rid, pid, m, lo, hi, dlo, s = trs[0]
            g.remote_dma(out_ap=T.rx[:, dlo:dlo + hi - lo], in_ap=src[:, lo:hi], remote_sem=T.sem[s], local_sem=T.sem.sent,
                         pid=pid, routing_id=rid, dma_engine_mask=m)
        else:
            g.remote_dma_fused([RemoteDMATransfer(dst_ids=[DstId(rid=rid, pnc=pid)], dma_engine_mask=m, remote_sem=T.sem[s],
                                                  src=src[:, lo:hi], dst=T.rx[:, dlo:dlo + hi - lo])
                                for d, rid, pid, m, lo, hi, dlo, s in trs], local_sem=T.sem.sent)
    g.wait_ge(T.sem.sent, sent)


def rank_program(g, core, T, topo):
    if "p" not in _CACHE:
        _CACHE["p"] = _plan(T, topo)
    P = _CACHE["p"]
    calls, expect = P["calls"], P["expect"]
    j = T.rank_of(core)
    if j is None:
        if core in calls:
            _issue(g, core, T, topo, calls[core], T.rx)
        return
    sem = T.sem
    pieces, loads, pload, units, ownp = P["pieces"][j], P["loads"][j], P["pload"][j], P["units"][j], P["ownp"][j]

    g.scalar.dma_start(T.f1s[:], T.f1[:]).then_inc(sem.lf1, 16)
    for n, (lo, hi) in enumerate(loads):
        g.sync.dma_start(T.xs[:, TK * lo:TK * hi], T.x[:, TK * lo:TK * hi]).then_inc(sem["lx%d" % n], 16)
        g.scalar.dma_start(T.ts[:, TK * lo:TK * hi], T.t[:, TK * lo:TK * hi]).then_inc(sem["lt%d" % n], 16)
    g.sync.dma_start(T.f2s[:], T.f2[:]).then_inc(sem.lf2, 16)

    g.tensor.wait_ge(sem.lf1, 16)
    seen = set()
    for p, (lo, hi) in enumerate(pieces):
        n = pload[p]
        if n not in seen:
            seen.add(n)
            g.tensor.wait_ge(sem["lx%d" % n], 16)
            g.vector.wait_ge(sem["lt%d" % n], 16)
        ps, w = T["ps%d" % p], TK * (hi - lo)
        g.tensor.matmul(ps[:, 0:w], T.f1s[:], T.xs[:, TK * lo:TK * hi], True, True).then_inc(sem["mm%d" % p], 1)
        g.vector.wait_ge(sem["mm%d" % p], 1)
        g.vector.tensor_tensor(T.u[:, TK * lo:TK * hi], ps[:, 0:w], T.ts[:, TK * lo:TK * hi], AluOpType.mult).then_inc(sem["u%d" % p], 1)

    _issue(g, core, T, topo, calls[core], T.u)

    g.tensor.wait_ge(sem.lf2, 16)
    queues = [g.sync, g.scalar]
    bank, ym = [len(pieces)], [0]

    def next_bank():
        b = bank[0]
        bank[0] += 1
        if b >= NB:
            b -= NB
            g.tensor.wait_ge(sem["u%d" % b], 1)
        return T["ps%d" % b]

    for n, (blocks, blockwise) in enumerate(units):
        lo, hi = TK * blocks[0], TK * (blocks[-1] + 1)
        copies = 0
        if blockwise:
            for r in blocks:
                py = next_bank()
                k = ym[0]
                ym[0] += 1
                g.tensor.wait_ge(sem["arr%d" % r], expect[core]["arr%d" % r])
                g.tensor.matmul(py[:, 0:TK], T.f2s[:], T.rx[:, TK * r:TK * r + TK], True, True).then_inc(sem["ym%d" % k], 1)
                g.vector.wait_ge(sem["ym%d" % k], 1)
                g.vector.tensor_copy(T.ys[:, TK * r:TK * r + TK], py[:, 0:TK]).then_inc(sem["yc%d" % n], 1)
                copies += 1
        else:
            py = next_bank()
            k = ym[0]
            ym[0] += 1
            for r in blocks:
                if r != j:
                    g.tensor.wait_ge(sem["arr%d" % r], expect[core]["arr%d" % r])
            if j in blocks:
                g.tensor.wait_ge(sem["u%d" % ownp], 1)
                for r in blocks:
                    rhs = T.u if r == j else T.rx
                    g.tensor.matmul(py[:, TK * r - lo:TK * r - lo + TK], T.f2s[:], rhs[:, TK * r:TK * r + TK], True, True).then_inc(sem["ym%d" % k], 1)
                done = len(blocks)
            else:
                g.tensor.matmul(py[:, 0:hi - lo], T.f2s[:], T.rx[:, lo:hi], True, True).then_inc(sem["ym%d" % k], 1)
                done = 1
            g.vector.wait_ge(sem["ym%d" % k], done)
            g.vector.tensor_copy(T.ys[:, lo:hi], py[:, 0:hi - lo]).then_inc(sem["yc%d" % n], 1)
            copies = 1
        q = queues[n % 2]
        q.wait_ge(sem["yc%d" % n], copies)
        q.dma_start(T.y[:, lo:hi], T.ys[:, lo:hi]).then_inc(sem["st%d" % n], 16)
    for n in range(len(units)):
        queues[n % 2].wait_ge(sem["st%d" % n], 16)
